import numpy as np, ml_dtypes
CORES = [6,15,38,47]
N = 4
BF = ml_dtypes.bfloat16
def gentries(a):
    return np.ascontiguousarray(a.reshape(8, 16, -1).transpose(0, 2, 1)).reshape(8, -1)
def gtable(e):
    e = np.asarray(e); return np.ascontiguousarray(e.reshape(8, -1, 16).transpose(0, 2, 1)).reshape(128, -1).astype(np.int32)
W, C, M, LO, SH, RO = 4096, 64, 64, 16, 5, 4
def parts(rng):
    return rng.integers(0, 256, (N, 8, 16, W)), rng.integers(0, W, (N, 8, C, M)), rng.integers(LO, M + 1, (N, 8, C)), rng.integers(1000, 1800, (N, 8, C))
def pack(bank, s, n, t):
    return {"bank": np.ascontiguousarray(bank.reshape(N, 128, W)).astype(np.float32).astype(BF), "arms": np.stack([gtable(a.transpose(0, 2, 1).reshape(8, -1)) for a in s]),
            "len0": np.stack([gtable(a) for a in n]), "th": np.stack([gtable(a) for a in t])}
def setup_inputs(rng):
    return pack(*parts(rng))
def setup_inputs_ties(rng):
    bank, s, n, t = parts(rng); pool = rng.integers(0, 256, (1, 8, 16, 3)); pool[:, 2, :, 0] = 0; pool[:, 2, :, 1:] = 255
    pick = rng.integers(0, 3, (N, 8, 1, W)); pick[0::2, 6] = 1
    pick[1::2, 6] = np.where(rng.random((N // 2, 1, W)) < 0.03, pick[1::2, 6], 1)
    bank = np.take_along_axis(np.repeat(pool, N, axis=0), pick, 3)
    far = np.add.reduce(np.abs(pool[0][:, :, :, None] - pool[0][:, :, None, :]), axis=1)
    i = rng.integers(0, 3, (N, 8, C)); j = rng.integers(0, 3, (N, 8, C))
    n[:, 4] = M; z = np.add.accumulate(s[:, 4], axis=2) & (W - 1); h = (((z * z) >> SH) + s[:, 4]) & (W - 1)
    c = np.arange(C); bank[:, 4] = pool[:, 4, :, :1]
    bank[np.arange(N)[:, None], 4, 0, h[:, c, M - 1 - c % 2]] = pool[0, 4, 0, 0] ^ 1
    return pack(bank, s, n, far[np.arange(8)[None, :, None], i, j] + rng.integers(0, 2, (N, 8, C)))
def setup_inputs_ends(rng):
    bank, s, n, t = parts(rng); e = rng.integers(0, W, (3, C))
    bank[:, 5] = bank[0, 5].copy(); bank[0::2, 7][:, :, e[1]] = 0; bank[1::2, 7][:, :, e[1]] = 255
    u = (rng.random((N, 16, C)) * rng.integers(1, 56, C)).astype(np.int64)
    bank[0::2, 6][:, :, e[2]] = u[0::2]; bank[1::2, 6][:, :, e[2]] = 255 - u[1::2]
    np.put_along_axis(s[:, 5], n[:, 5, :, None] - 1, e[0][None, :, None], 2)
    np.put_along_axis(s[:, 6], n[:, 6, :, None] - 1, e[2][None, :, None], 2)
    np.put_along_axis(s[:, 7], n[:, 7, :, None] - 1, e[1][None, :, None], 2)
    last = np.take_along_axis(s, n[..., None] - 1, 3)[..., 0]; end = np.take_along_axis(bank, last[:, :, None, :], 3)
    t = np.add.reduce(np.abs(end - np.roll(end, 1, axis=0)), axis=2) + rng.integers(0, 2, (N, 8, C))
    t[:, 0] = 0; t[:, 1] = 4081
    return pack(bank, s, n, t)
def setup_inputs_lengths(rng):
    bank, s, n, t = parts(rng)
    n[:, 0] = LO; n[:, 1] = M
    x = rng.integers(LO + 1, M - LO, C); n[:, 2] = x
    n[1::2, 2] = M - x + rng.integers(-1, 2, (N // 2, C)); t[:, 2] = 4081
    n[:, 3] = M // 2 + rng.integers(-1, 2, (N, C)); t[:, 3] = 0
    n[:, 4] = rng.choice(np.array([LO, LO + 1, M - 1, M]), (N, C)); t[:, 4] = rng.choice(np.array([0, 4081]), (N, C))
    return pack(bank, s, n, t)
def setup_inputs_codes(rng):
    bank, s, n, t = parts(rng)
    s[:, 0] = W - 1; n[:, 0] = np.maximum(n[:, 0], rng.integers(LO, M + 1, (N, C))); n[:, 0, :4] = M
    bank[:, 0] = rng.integers(128, 256, (N, 16, W)); t[:, 0] = rng.integers(500, 900, (N, C))
    z = (M * (W - 1) - 1) & (W - 1); bank[:, 0, :, (((z * z) >> SH) + W - 1) & (W - 1)] = 0
    s[:, 1] = 0; s[:, 2] = s[:, 2] & (W - 2); s[:, 3] = s[:, 3] | 1
    s[:, 4] = s[:, 4, :, :1].copy(); s[:, 6] = rng.choice(np.array([0, 1, W - 2, W - 1]), (N, C, M))
    s[:, 5, :, LO - 1:] = 0; n[:, 5] = M
    s[:, 7] = rng.integers(W - 16, W, (N, C, M)); bank[:, 7] = rng.integers(192, 256, (N, 16, W)); t[:, 7] = rng.integers(250, 450, (N, C))
    bank[:, 7][:, :, (((W - 1) * (W - 1) >> SH) + np.arange(W - 16, W)) & (W - 1)] = 0
    return pack(bank, s, n, t)
def setup_inputs_spread(rng):
    bank, s, n, t = parts(rng)
    bank = np.minimum((np.exp2(rng.integers(0, 9, (N, 8, 1, W))) * rng.random((N, 8, 16, W))).astype(np.int64), 255)
    s = (W * rng.random((N, 8, C, M)) ** rng.choice(np.array([1, 2, 5]), (N, 8, C, 1))).astype(np.int64)
    n = np.minimum(LO + ((M + 1 - LO) * rng.random((N, 8, C)) ** rng.choice(np.array([1, 3]), (N, 8, 1))).astype(np.int64), M)
    t = np.minimum(np.exp2(12 * rng.random((N, 8, C))).astype(np.int64), 4081)
    return pack(bank, s, n, t)
def check_inputs(d):
    bad = []; v = np.asarray(d["bank"]).astype(np.float32)
    if not np.all((v >= 0) & (v <= 255) & (v == np.floor(v))): bad.append("bank holds whole numbers from 0 to 255")
    for k, lo, hi in (("arms", 0, W - 1), ("len0", LO, M), ("th", 0, 4081)):
        if np.min(d[k]) < lo or np.max(d[k]) > hi: bad.append("range of " + k)
    return bad
def reference(bank, arms, len0, th):
    B = bank.astype(np.float32).astype(np.int32).reshape(N, 8, 16, W)
    S = np.stack([gentries(a) for a in arms]).astype(np.int64).reshape(N, 8, M, C).transpose(0, 1, 3, 2)
    n = np.stack([gentries(a) for a in len0]).astype(np.int64); T = np.stack([gentries(a) for a in th]).astype(np.int64)
    A = np.zeros((N, 8, C), np.int64); k = np.arange(M)
    for t in range(RO):
        d = 1 + t % (N - 1)
        last = np.take_along_axis(S, n[..., None] - 1, 3)[..., 0]
        E = np.take_along_axis(B, last[:, :, None, :], 3)
        near = np.add.reduce(np.abs(E - np.roll(E, d, axis=0)), axis=2) < T
        S2 = np.where(near[..., None], np.roll(S, d, axis=0), S); n2 = np.where(near, np.roll(n, d, axis=0), n)
        L = np.minimum(n + n2, M)
        back = np.clip((n + n2)[..., None] - 1 - k, 0, M - 1)
        Q = np.where(k < n[..., None], S, np.take_along_axis(S2, back, 3) ^ 1)
        Q = np.where(k < L[..., None], Q, 0)
        z = (np.add.accumulate(Q, axis=3) + A[..., None]) & (W - 1)
        h = (((z * z) >> SH) + Q) & (W - 1)
        R = np.take_along_axis(B, h.reshape(N, 8, 1, C * M), 3).reshape(N, 8, 16, C, M)
        D = np.add.reduce(np.abs(R[..., 1:] - R[..., :-1]), axis=2)
        ok = (k[1:] >= LO) & (k[1:] < L[..., None])
        b = 1 + np.argmax(np.where(ok, D, -1), axis=3)
        A = A + np.take_along_axis(np.add.reduce(R, axis=2), b[..., None], 3)[..., 0]
        S = np.where(k < b[..., None], Q, 0); n = b
    ys = np.stack([gtable(a.transpose(0, 2, 1).reshape(8, -1)) for a in S]).astype(np.float32)
    yn = np.stack([gtable(a) for a in n]).astype(np.float32); ya = np.stack([gtable(a) for a in A]).astype(np.float32)
    return {"ys": ys, "yn": yn, "ya": ya}

@@ -1,0 +1,543 @@
+import math
+from concourse.bass import DstId, RemoteDMATransfer
+from concourse.mybir import AluOpType as OP, AxisListType as AX, ActivationFunctionType as AF
+
+RO, NQ, WW = 4, 4, 280
+SCRATCH = {"bk": ("sbuf", [128, 4096], "bfloat16"), "win": ("sbuf", [128, RO * NQ * WW], "float32"),
+           "dg": ("sbuf", [128, 2048], "float16"), "nih": ("sbuf", [128, 128], "float16")}
+for _n, _w in dict(ai=256, li=4, ti=4, par=256, pi=4).items():
+    SCRATCH[_n] = ("sbuf", [128, _w], "int32")
+for _n, _w in dict(ysb=256, ynb=4, yab=4, sg=256, vp=256, thf=4, thm=64, pf=4, col=144, d16=16, i32=128, kn=48, kh=48,
+                   c2=2, c3=2, zer=48, m15=52).items():
+    SCRATCH[_n] = ("sbuf", [128, _w], "float32")
+for _n, _w in dict(cg=128, ib=128, nib=128, big=128, one=128, non=128, zsel=144, kk=96, kl=96).items():
+    SCRATCH[_n] = ("sbuf", [128, _w], "bfloat16")
+for _q in range(NQ):
+    SCRATCH.update({
+        "sm%d" % _q: ("sbuf", [128, 32], "float32"),
+        "mm%d" % _q: ("sbuf", [128, 32], "bfloat16"),
+        "of%d" % _q: ("sbuf", [128, 104], "uint16"),
+        "pen%d" % _q: ("sbuf", [128, 48], "bfloat16"),
+        "gj%d" % _q: ("sbuf", [128, 768], "float16"),
+        "f%d" % _q: ("sbuf", [128, 576], "float32"),
+        "xi%d" % _q: ("sbuf", [128, 128], "int32"),
+        "rx%d" % _q: ("sbuf", [128, 1552], "bfloat16"),
+        "ps%d" % _q: ("psum", [128, 512], "float32"),
+        "pd%d" % _q: ("psum", [128, 512], "float32"),
+    })
+ENG = ["v", "s", "p", "g"]
+SEMAPHORES = (["cv", "cs", "cp", "cg", "loc", "la", "lb", "ll", "lt", "o0", "o1", "o2", "o3"]
+              + ["a%s%d%d" % (x, t, q) for x in "re" for t in range(RO) for q in range(NQ)])
+
+COST = dict(cy=1.04, pcy=0.52, gam=1.56, fix=25.0, hop=70.0, rem=2800.0, bank=6000.0, add=0.0)
+GUESS = [COST, dict(COST, cy=0.83, pcy=0.42, gam=1.04, fix=0.0, hop=40.0, rem=2000.0, bank=4000.0),
+         dict(COST, cy=1.25, pcy=0.62, gam=2.08, hop=120.0, rem=3500.0)]
+OPT = dict(pen="s", gate="s", dist="mm", red="v", merge=0, split=1, js=2, two=0, skew=2500.0, slack=45.0, iters=12000, temp=0.002)
+S = 2.0 ** -21
+
+
+def R(name, lo, hi, step=1):
+    return (name, lo, hi, step)
+
+
+def build_ops(C, O):
+    ops = []
+    tag = [0]
+
+    def add(eng, call, reads, writes, cost, after=(), sem=None, lat=0.0, soft=()):
+        ops.append(dict(i=len(ops), eng=eng, call=call, reads=[r for r in reads if isinstance(r, tuple)], writes=writes,
+                        cost=cost, after=list(after), sem=sem, lat=lat, tag=tag[0], soft=set(soft)))
+        return len(ops) - 1
+
+    def n(r):
+        return len(range(r[1], r[2], r[3]))
+
+    def two(r):
+        return SCRATCH[r[0]][2] in ("bfloat16", "float16", "uint16")
+
+    def vc(x):
+        return (max(64.0, x) if not C["add"] else C["add"] + x) * C["cy"] + C["fix"]
+
+    def ts(out, in0, a, b, op0, op1=None):
+        c = vc(n(out) * (0.5 if two(out) and two(in0) else 1))
+        return add("v", ("ts", out, in0, a, b, op0, op1), [in0, a, b], [out], c)
+
+    def tt(out, a, b, op):
+        ps = SCRATCH[a[0]][0] == "psum" or SCRATCH[b[0]][0] == "psum"
+        return add("v", ("tt", out, a, b, op), [a, b], [out], vc(n(out) * (1 if ps else 2)))
+
+    def cp(out, a):
+        return add("v", ("cp", out, a), [a], [out], vc(n(out)))
+
+    def red(out, a, op):
+        return add("v", ("red", out, a, op), [a], [out], vc(n(a)))
+
+    def scan(out, a, b, init, op0, op1):
+        return add("v", ("scan", out, a, b, init, op0, op1), [a, b, init], [out], vc(n(out)))
+
+    def act(out, a, f, bias=0.0, scale=1.0, acc=None):
+        return add("s", ("act", out, a, f, bias, scale, acc), [a, bias, scale], [out] + ([acc] if acc else []),
+                   vc(n(out)) + (20 if acc else 0))
+
+    def gat(eng, out, w, off):
+        return add(eng, ("gat", out, w, off), [w, off], [out], n(out) * C["gam"] * C["cy"] + 65)
+
+    def iota(out, pat, base, ch):
+        return add("g", ("iota", out, pat, base, ch), [], [out], 160 + 2 * n(out) * C["cy"])
+
+    def mm(parts, after=()):
+        c = sum(max(64, n(p[2])) * (4 if SCRATCH[p[2][0]][2] == "float32" else 1) for p in parts) * C["pcy"] + C["fix"]
+        return add("p", ("mm", parts), [p[1] for p in parts] + [p[2] for p in parts], [p[0] for p in parts], c, after)
+
+    def dma(queue, sem, out, a, reads, writes, lat, soft=()):
+        return add(queue, ("dma", out, a), reads, writes, 60.0, sem=(sem, 16), lat=lat, soft=soft)
+
+    def send(t, parts):
+        i = add("g", ("send", t, parts), [p[0] for p in parts], [], 300.0 + 30 * len(parts))
+        for p in parts:
+            add("r", None, [], [p[1]], 0.0, after=[i], sem=(p[2], -len(parts)), lat=C["rem"] - 500 + 6 * n(p[0]) * len(parts))
+
+    i = dma("y", "la", R("ai", 0, 256), ("arms", 0, 256), [], [R("ai", 0, 256)], 2300.0)
+    dma("y", "lb", R("bk", 0, 4096), ("bank", 0, 4096), [], [R("bk", 0, 4096)], C["bank"], soft=[i])
+    i = dma("s", "ll", R("li", 0, 4), ("len0", 0, 4), [], [R("li", 0, 4)], 2100.0)
+    dma("s", "lt", R("ti", 0, 4), ("th", 0, 4), [], [R("ti", 0, 4)], 2100.0, soft=[i])
+    iota(R("col", 0, 144), [[1, 144]], 0, 0)
+    iota(R("pi", 0, 1), [[0, 1]], 0, 1)
+    iota(R("pf", 0, 1), [[0, 1]], 0, 1)
+    iota(R("cg", 0, 128), [[1, 8], [0, 16]], 0, 0)
+    iota(R("kn", 0, 48), [[-1, 48]], 15, 0)
+    iota(R("c2", 0, 2), [[-132, 2]], 132, 0)
+    ts(R("pi", 1, 2), R("pi", 0, 1), 4, None, OP.arith_shift_right)
+    ts(R("pi", 2, 3), R("pi", 0, 1), 15, None, OP.bitwise_and)
+    cp(R("pf", 1, 3), R("pi", 1, 3))
+    ts(R("pf", 3, 4), R("pf", 1, 2), 16.0, 15.0, OP.mult, OP.add)
+    ts(R("d16", 0, 16), R("col", 0, 16), R("pf", 2, 3), None, OP.is_equal)
+    ts(R("i32", 0, 128), R("col", 0, 128), R("pf", 0, 1), None, OP.is_equal)
+    ts(R("nih", 0, 128), R("col", 0, 128), R("pf", 0, 1), -1.0, OP.is_equal, OP.mult)
+    act(R("ib", 0, 128), R("i32", 0, 128), AF.Copy)
+    act(R("nib", 0, 128), R("i32", 0, 128), AF.Copy, scale=-1.0)
+    act(R("big", 0, 128), R("i32", 0, 128), AF.Copy, scale=0.25 if O["pen"] == "s" else -0.25)
+    ts(R("one", 0, 128), R("cg", 0, 128), R("pf", 1, 2), None, OP.is_equal)
+    if O["dist"] == "mm":
+        act(R("non", 0, 128), R("one", 0, 128), AF.Copy, scale=-1.0)
+    ts(R("zsel", 0, 144), R("col", 0, 144), R("pf", 3, 4), S, OP.is_equal, OP.mult)
+    act(R("kk", 0, 48), R("col", 16, 64), AF.Copy, scale=1.0 / 128)
+    act(R("kk", 48, 96), R("col", 16, 64), AF.Identity, scale=-S, bias=63 * S)
+    act(R("kl", 0, 48), R("col", 16, 64), AF.Copy, scale=0.0)
+    act(R("kl", 48, 96), R("col", 16, 64), AF.Identity, scale=-S, bias=63 * S)
+    act(R("kh", 0, 48), R("col", 16, 64), AF.Identity, bias=0.5)
+    act(R("c3", 0, 2), R("col", 0, 2), AF.Identity, scale=2.0 - 1.0 / 128, bias=1.0 / 128)
+    act(R("zer", 0, 48), R("col", 0, 48), AF.Copy, scale=0.0)
+    act(R("m15", 0, 3), R("col", 0, 3), AF.Copy, scale=0.0)
+    act(R("m15", 3, 52), R("col", 0, 49), AF.Identity, scale=0.0, bias=-1.5 * S)
+    for i in range(16):
+        ts(R("dg", 128 * i, 128 * i + 128), R("nih", 0, 128), R("d16", i, i + 1), None, OP.mult)
+    for w in range(RO * NQ + 1):
+        b = w * WW
+        tag[0] = max(w - 1, 0)
+        spans = [(max(b - 52, 0), min(b + 32, RO * NQ * WW))] + ([(b + 96, b + 144)] if w < RO * NQ else [])
+        for lo, hi in spans:
+            if w < NQ:
+                act(R("win", lo, hi), R("col", 0, hi - lo), AF.Copy, scale=0.0)
+            else:
+                iota(R("win", lo, hi), [[0, hi - lo]], 0, 0)
+    tag[0] = 0
+    cp(R("ysb", 0, 256), R("ai", 0, 256))
+    dma("y", "o0", ("ys", 0, 64), R("ysb", 0, 64), [R("ysb", 0, 64)], [], 2200.0)
+    ts(R("par", 0, 256), R("ai", 0, 256), 1, None, OP.bitwise_and)
+    ts(R("sg", 0, 256), R("par", 0, 256), -0.5, None, OP.add)
+    act(R("vp", 0, 256), R("ysb", 0, 256), AF.Identity, bias=1.5)
+    tt(R("sg", 0, 256), R("sg", 0, 256), R("vp", 0, 256), OP.mult)
+    act(R("sg", 0, 256), R("sg", 0, 256), AF.Identity, bias=-0.25)
+    cp(R("thf", 0, 4), R("ti", 0, 4))
+    for q in range(NQ):
+        b = q * WW
+        f, sm, of = "f%d" % q, "sm%d" % q, "of%d" % q
+        nn = R("win", b + 28, b + 29)
+        cp(nn, R("li", q, q + 1))
+        ts(R(f, 400, 464), R("col", 0, 64), 1.0, nn, OP.add, OP.is_equal)
+        tt(R(f, 464, 528), R(f, 400, 464), R("ysb", q, 256, 4), OP.mult)
+        act(R(f, 160, 224), R(f, 464, 528), AF.Copy, acc=R(sm, 24, 25))
+        cp(R(of, 100, 101), R(sm, 24, 25))
+        gat("s" if q % 2 else "v", R("win", b + 12, b + 28), R("bk", 0, 4096), R(of, 100, 101))
+        ts(R(f, 336, 400), R("col", 0, 64), nn, None, OP.is_lt)
+        tt(R("win", b + 32, b + 96), R(f, 336, 400), R("sg", q, 256, 4), OP.mult)
+        act(R("thm", 16 * q, 16 * q + 16), R("d16", 0, 16), AF.Copy, scale=R("thf", q, q + 1))
+        act(R(f, 224, 239), R("ysb", q, 60, 4), AF.Identity, bias=-136.5 * S, scale=S, acc=R(sm, 26, 27))
+        act(R(f, 52, 53), R("vp", 60 + q, 61 + q), AF.Copy, scale=S)
+        act(R(f, 104, 105), R("vp", 60 + q, 61 + q), AF.Identity, bias=-131120.0, scale=32.0)
+        act(R(f, 272, 288), R("col", 0, 16), AF.Identity, scale=0.0, bias=-1.0)
+        act(R(sm, 22, 24), R("c3", 0, 2), AF.Identity, scale=nn, bias=1.5 * S)
+    for name, lo, hi in (("ar0", 28, 96), ("ae0", 12, 28)):
+        send(0, [(R("win", q * WW + lo, q * WW + hi), R("win", q * WW + lo + 132, q * WW + hi + 132), "%s%d" % (name, q))
+                 for q in range(NQ)])
+    for t in range(RO):
+        for q in range(NQ):
+            tag[0] = t * NQ + q
+            b = (t * NQ + q) * WW
+            b2 = b + NQ * WW
+            f, sm, of, ps = "f%d" % q, "sm%d" % q, "of%d" % q, "ps%d" % q
+            mx_, gj, xi, rx, pen = "mm%d" % q, "gj%d" % q, "xi%d" % q, "rx%d" % q, "pen%d" % q
+            pa, pb = "pd%d" % (2 * (q % 2)), "pd%d" % (2 * (q % 2) + 1)
+            nn, ns = R("win", b + 28, b + 29), R("win", b + 160, b + 161)
+            e, es = R("win", b + 12, b + 28), R("win", b + 144, b + 160)
+            last = t == RO - 1
+            if O["dist"] == "mm":
+                tt(R(mx_, 0, 16), e, es, OP.max)
+                tt(R(mx_, 16, 32), e, es, OP.min)
+                mm([(R(ps, 64, 80), R("one", 0, 128), R(mx_, 0, 16), True, False),
+                    (R(ps, 64, 80), R("non", 0, 128), R(mx_, 16, 32), False, True)])
+            else:
+                tt(R(mx_, 0, 16), e, es, OP.subtract)
+                act(R(mx_, 16, 32), R(mx_, 0, 16), AF.Abs)
+                mm([(R(ps, 64, 80), R("one", 0, 128), R(mx_, 16, 32), True, True)])
+            ts(R(sm, 16, 18), R("c2", 0, 2), ns, nn, OP.add, OP.subtract)
+            lt = tt(R(sm, 0, 16), R(ps, 64, 80), R("thm", 16 * q, 16 * q + 16), OP.is_lt)
+            if O["red"] == "v":
+                red(R(sm, 18, 19), R(sm, 0, 16), OP.add)
+            else:
+                act(R(sm, 0, 16), R(sm, 0, 16), AF.Copy, acc=R(sm, 18, 19))
+            ts(R(sm, 20, 22), R(sm, 16, 18), R(sm, 18, 19), R(sm, 23, 24), OP.mult, OP.add)
+            ts(R(of, 0, 48), R("kn", 0, 48), R(sm, 20, 21), None, OP.add)
+            if O["pen"] == "s":
+                act(R(pen, 0, 48), R("kh", 0, 48), AF.Sign, bias=R(sm, 21, 22), scale=-1.0)
+            else:
+                ts(R(pen, 0, 48), R("kh", 0, 48), R(sm, 21, 22), None, OP.is_gt)
+            js = O["js"]
+            for a in range(js):
+                gat("v", R(gj, 768 // js * a, 768 // js * (a + 1)), R("win", b, b + 276), R(of, 48 // js * a, 48 // js * (a + 1)))
+            mm([(R(ps, 0, 64), R("i32", 0, 128), R("win", b + 32, b + 96), True, False)], after=[lt])
+            mm([(R(ps, 16, 64), R("dg", 128 * i, 128 * i + 128), R(gj, i, 768, 16), False, i == 15) for i in range(16)])
+            act(R(f, 53, 101), R(ps, 16, 64), AF.Abs, bias=0.5 * S, scale=2.0 * S)
+            scan(R(ps, 128 - t, 177), R(f, 52 - t, 101), R("m15", 3 - t, 52), R(sm, 26, 27), OP.add, OP.add)
+            act(R(f, 105, 153), R(f, 53, 101), AF.Identity, bias=-131120.0, scale=32.0 / S)
+            ts(R(f, 160, 209), R(ps, 128, 177), 1.5 * 2.0 ** 35 * S, 1.5 * 2.0 ** 35 * S, OP.add, OP.subtract)
+            tt(R(f, 216, 265), R(ps, 128, 177), R(f, 160, 209), OP.subtract)
+            act(R(ps, 192, 241), R(f, 216, 265), AF.Square, bias=2047.5, scale=1.0 / S)
+            tt(R(xi, 0, 49), R(ps, 192, 241), R(f, 104, 153), OP.add)
+            ts(R(xi, 64, 113), R(xi, 0, 49), 5, 4095, OP.arith_shift_right, OP.bitwise_and)
+            prev = cp(R(of, 48, 97), R(xi, 64, 113))
+            if O["split"]:
+                gat("s", R(rx, 0, 416), R("bk", 0, 4096), R(of, 48, 74))
+                gat("s", R(rx, 416, 784), R("bk", 0, 4096), R(of, 74, 97))
+            else:
+                gat("s", R(rx, 0, 784), R("bk", 0, 4096), R(of, 48, 97))
+            if not last:
+                prev = mm([(R(ps, 368, 416), R("i32", 0, 128), R(f, 52, 100), True, False),
+                           (R(ps, 368, 416), R("ib", 0, 128), R("kk", 0, 48), False, True)], after=[prev])
+            else:
+                act(R(f, 400, 403), R(f, 49, 52), AF.Identity, bias=2730.5 * S, scale=-1.0, acc=R(sm, 24, 25))
+                ts(R(f, 48, 49), R(sm, 24, 25), 1.5 * 2.0 ** 37 * S, 1.5 * 2.0 ** 37 * S, OP.add, OP.subtract)
+                act(R(f, 464, 512), R(f, 53, 101), AF.Identity, bias=-1.5, scale=1.0 / S)
+            for pdx, lo in ((pa, 0), (pb, 384)):
+                mm([(R(pdx, 0, 384), R("ib", 0, 128), R(rx, lo + 16, lo + 400), True, False),
+                    (R(pdx, 0, 384), R("nib", 0, 128), R(rx, lo, lo + 384), False, True)])
+                act(R(rx, 784 + lo, 784 + lo + 384), R(pdx, 0, 384), AF.Abs, scale=64.0)
+            kt = "kl" if last else "kk"
+            if O["merge"]:
+                mm([(R(ps, 256, 352), R("ib", 0, 128), R(kt, 0, 96), True, False),
+                    (R(ps, 304, 352), R("big", 0, 128), R(pen, 0, 48), False, False)], after=[prev])
+                mm([(R(ps, 256, 352), R("zsel", 15 - i, 143 - i), R(rx, 16 + i, 1552, 16), False, i == 15) for i in range(16)])
+            else:
+                tg = mm([(R(ps, 256, 304), R("ib", 0, 128), R(kt, 0, 48), True, False)]
+                        + [(R(ps, 256, 304), R("zsel", 15 - i, 143 - i), R(rx, 16 + i, 784, 16), False, i == 15) for i in range(16)],
+                        after=[prev])
+                mm([(R(ps, 304, 352), R("ib", 0, 128), R(kt, 48, 96), True, False),
+                    (R(ps, 304, 352), R("big", 0, 128), R(pen, 0, 48), False, False)], after=[tg])
+                mm([(R(ps, 304, 352), R("zsel", 15 - i, 143 - i), R(rx, 784 + i, 1552, 16), False, i == 15) for i in range(16)])
+            scan(R(f, 288, 336), R(ps, 304, 352), R("zer", 0, 48), 0.0, OP.max, OP.add)
+            top = R(f, 335, 336)
+            n2 = R("ynb", q, q + 1) if last else R("win", b2 + 28, b2 + 29)
+            act(R(f, 336, 400), R(f, 272, 336), AF.Sign, bias=top, scale=-1.0, acc=n2)
+            if not last:
+                act(R(sm, 22, 24), R("c3", 0, 2), AF.Identity, scale=n2, bias=1.5 * S)
+                scan(R(f, 528, 576), R(f, 351, 399), R(ps, 368, 416), 0.0, OP.max, OP.min)
+                ts(R(of, 100, 101), R(f, 575, 576), R(sm, 22, 23), 1.0 / S, OP.subtract, OP.mult)
+                gat(O["gate"], R("win", b2 + 12, b2 + 28), R("bk", 0, 4096), R(of, 100, 101))
+                tt(R("win", b2 + 32, b2 + 96), R(ps, 0, 64), R(f, 336, 400), OP.mult)
+                for x, lo, hi in ((("r", 28, 96), ("e", 12, 28)) if O["two"] else (("r", 12, 96),)):
+                    send(t + 1, [(R("win", b2 + lo, b2 + hi), R("win", b2 + lo + 132, b2 + hi + 132), "a%s%d%d" % (x, t + 1, q))])
+                scan(R(f, 4 - t, 52 - t), R(f, 351, 399), R(ps, 256, 304), 0.0, OP.max, OP.min)
+            else:
+                tt(R("ysb", 64 + q, 256, 4), R(f, 464, 512), R(f, 352, 400), OP.mult)
+                ts(R(f, 404, 452), R(ps, 304, 352), top, None, OP.is_equal)
+                tt(R(f, 0, 48), R(ps, 256, 304), R(f, 404, 452), OP.mult)
+                act(R(f, 104, 156), R(f, 0, 52), AF.Copy, scale=1.0 / S, acc=R("yab", q, q + 1))
+    tag[0] = -1
+    dma("y", "o1", ("ys", 64, 256), R("ysb", 64, 256), [R("ysb", 64, 256)], [], 2300.0)
+    dma("y", "o2", ("yn", 0, 4), R("ynb", 0, 4), [R("ynb", 0, 4)], [], 2100.0)
+    dma("s", "o3", ("ya", 0, 4), R("yab", 0, 4), [R("yab", 0, 4)], [], 2100.0)
+    return ops
+
+
+def link(ops):
+    hist = {}
+    for o in ops:
+        deps = set(o["after"])
+        for kind, regs in (("r", o["reads"]), ("w", o["writes"])):
+            for r in regs:
+                for (j, k2, lo, hi) in hist.get(r[0], []):
+                    if lo < r[2] and r[1] < hi and (kind == "w" or k2 == "w"):
+                        deps.add(j)
+        for kind, regs in (("r", o["reads"]), ("w", o["writes"])):
+            for r in regs:
+                hist.setdefault(r[0], []).append((o["i"], kind, r[1], r[2]))
+        deps.discard(o["i"])
+        o["deps"] = deps
+        o["banks"] = sorted(set(r[0] for r in o["reads"] + o["writes"] if SCRATCH[r[0]][0] == "psum"))
+
+
+def greedy(ops, hop, O):
+    users = [[] for _ in ops]
+    for o in ops:
+        for j in o["deps"] | o["soft"]:
+            users[j].append(o["i"])
+    for o in reversed(ops):
+        own = -O["skew"] * (o["tag"] % NQ) if o["tag"] >= (RO - 1) * NQ else -1e9
+        o["prio"] = o["cost"] + o["lat"] + hop + max([ops[u]["prio"] for u in users[o["i"]] if ops[u]["tag"] >= 0] + [own])
+    free, bank, order = {}, {}, []
+    left = [len(o["deps"] | o["soft"]) for o in ops]
+    ready = [o for o in ops if not left[o["i"]]]
+
+    def start(o):
+        s = free.get(o["eng"], 0.0)
+        for j in list(o["deps"]) + [j for bk in o["banks"] for e2, j in bank.get(bk, {}).items() if e2 != o["eng"]]:
+            d = ops[j]
+            s = max(s, d["end"] + (0.0 if (d["eng"] == "p" and o["eng"] == "p") or o["eng"] == "r" else hop))
+        return s
+
+    while ready:
+        st = [(start(o), o) for o in ready]
+        s0, o0 = min(st, key=lambda x: (x[0], -x[1]["prio"]))
+        s1, o = max([x for x in st if x[1]["eng"] == o0["eng"] and x[0] <= s0 + O["slack"]], key=lambda x: x[1]["prio"])
+        free[o["eng"]] = s1 + o["cost"] if o["eng"] != "r" else 0.0
+        o["end"] = s1 + o["cost"] + o["lat"]
+        for bk in o["banks"]:
+            bank.setdefault(bk, {})[o["eng"]] = o["i"]
+        order.append(o["i"])
+        ready.remove(o)
+        for u in users[o["i"]]:
+            left[u] -= 1
+            if left[u] == 0:
+                ready.append(ops[u])
+    return order
+
+
+def improve(ops, order, costs, hops, iters, temp, seed=1):
+    n = len(ops)
+    eng = ["vspgyr".index(o["eng"]) for o in ops]
+    names = sorted(set(b for o in ops for b in o["banks"]))
+    banks = [[names.index(b) for b in o["banks"]] for o in ops]
+    anc = [0] * n
+    deps = []
+    for o in ops:
+        d = sorted(o["deps"] | o["soft"])
+        deps.append([j for j in d if j not in o["soft"] and not any(anc[k] >> j & 1 for k in d)])
+        for j in d:
+            anc[o["i"]] |= anc[j] | 1 << j
+    dep0 = [[j for j in deps[i] if (eng[i] == 2 and eng[j] == 2) or eng[i] == 5] for i in range(n)]
+    dep1 = [[j for j in deps[i] if j not in dep0[i]] for i in range(n)]
+
+    def run(seq, m):
+        cost, hop = costs[m], hops[m]
+        free, holder, end, why = [0.0] * 6, [-1] * 6, [0.0] * n, [-1] * n
+        bank = [[-1] * 3 for _ in names]
+        for i in seq:
+            e = eng[i]
+            s, w = (free[e], holder[e]) if e != 5 else (0.0, -1)
+            for j in dep1[i]:
+                if end[j] + hop > s:
+                    s, w = end[j] + hop, j
+            for j in dep0[i]:
+                if end[j] > s:
+                    s, w = end[j], j
+            for b in banks[i]:
+                bb = bank[b]
+                for e2 in (0, 1, 2):
+                    j = bb[e2]
+                    if e2 != e and j >= 0 and end[j] + hop > s:
+                        s, w = end[j] + hop, j
+                bb[e] = i
+            c = cost[i]
+            free[e] = s + c[0]
+            holder[e] = i
+            end[i] = s + c[0] + c[1]
+            why[i] = w
+        top = max(end)
+        i, path = end.index(top), []
+        while why[i] >= 0:
+            if not anc[i] >> why[i] & 1:
+                path.append((why[i], i))
+            i = why[i]
+        return top, path
+
+    state = [seed]
+
+    def rnd():
+        state[0] = (state[0] * 6364136223846793005 + 1442695040888963407) % 2 ** 64
+        return (state[0] >> 11) / 2.0 ** 53
+
+    nm = len(costs)
+    res = [run(order, m) for m in range(nm)]
+    base = [r[0] for r in res]
+    cur = best = float(nm)
+    keep = order
+    for it in range(iters):
+        path = res[int(rnd() * nm)][1]
+        if not path:
+            continue
+        p, o = path[int(rnd() * len(path))]
+        a, b = order.index(p), order.index(o)
+        if rnd() < 0.3:
+            a = max(0, a - int(rnd() * 12))
+            p = order[a]
+        mid = order[a:b + 1]
+        if rnd() < 0.5:
+            mv = [x for x in mid if x == o or anc[o] >> x & 1]
+            st = set(mv)
+            new = order[:a] + mv + [x for x in mid if x not in st] + order[b + 1:]
+        else:
+            mv = [x for x in mid if x == p or anc[x] >> p & 1]
+            st = set(mv)
+            new = order[:a] + [x for x in mid if x not in st] + mv + order[b + 1:]
+        r2 = [run(new, m) for m in range(nm)]
+        val = sum(r2[m][0] / base[m] for m in range(nm))
+        if val <= cur or rnd() < math.exp((cur - val) / (nm * temp * (1.0 - it / iters) + 1e-9)):
+            order, res, cur = new, r2, val
+            if val < best:
+                best, keep = val, new
+    return keep, [int(run(keep, m)[0]) for m in range(nm)]
+
+
+def plan(O=OPT, G=GUESS):
+    ops = build_ops(G[0], O)
+    link(ops)
+    seq = greedy(ops, G[0]["hop"], O)
+    seq, times = improve(ops, seq, [[(o["cost"], o["lat"]) for o in build_ops(c, O)] for c in G], [c["hop"] for c in G],
+                         O["iters"], O["temp"])
+    count, known, bank = {}, {}, {}
+    place = {i: k for k, i in enumerate(seq)}
+    for i in seq:
+        o = ops[i]
+        kn = known.setdefault(o["eng"], {})
+        waits = {}
+        need = set(o["deps"]) | set(j for bk in o["banks"] for e2, j in bank.get(bk, {}).items() if e2 != o["eng"])
+        for bk in o["banks"]:
+            bank.setdefault(bk, {})[o["eng"]] = i
+        if o["eng"] != "r":
+            for j in sorted(need, key=lambda j: -place[j]):
+                d = ops[j]
+                if d["eng"] == "p" and o["eng"] == "p":
+                    continue
+                s, v = d["done"]
+                if kn.get(s, 0) != v and (v < 0 or kn.get(s, 0) < v):
+                    waits[s] = v if v < 0 else max(v, waits.get(s, 0))
+                    kn[s] = v
+                    for s2, v2 in d["know"].items():
+                        if v2 < 0 or kn.get(s2, 0) < v2:
+                            kn[s2] = v2
+        o["waits"] = waits
+        o["know"] = {} if o["eng"] == "r" else dict(kn)
+        if o["sem"]:
+            o["done"] = o["sem"]
+        elif o["call"][0] == "send":
+            o["done"] = None
+        else:
+            count[o["eng"]] = count.get(o["eng"], 0) + 1
+            o["done"] = ("c" + o["eng"], count[o["eng"]])
+    return [ops[i] for i in seq], count, times
+
+
+PLAN = {}
+
+
+def rank_program(g, core, T, topo):
+    rank = T.rank_of(core)
+    if rank is None:
+        return
+    if "p" not in PLAN:
+        PLAN["p"] = plan()
+    order, count, _ = PLAN["p"]
+    nr = len(T.cores)
+    queue = {"v": g.vector, "s": g.scalar, "p": g.tensor, "g": g, "y": g.sync}
+
+    def peer(t, sign):
+        return T.cores[(rank + sign * (1 + t % (nr - 1))) % nr]
+
+    def ap(r):
+        if not isinstance(r, tuple):
+            return r
+        if len(r) == 4 and r[3] != 1:
+            return T[r[0]][:, r[1]:r[2]:r[3]]
+        return T[r[0]][:, r[1]:r[2]]
+
+    def value(s, v):
+        if v > 0:
+            return v
+        return len(topo.engines(peer(int(s[2]), -1), core)) // -v
+
+    sent = 0
+    for o in order:
+        if o["eng"] == "r":
+            continue
+        e = queue[o["eng"]]
+        for s, v in o["waits"].items():
+            e.wait_ge(T.sem[s], value(s, v))
+        c = o["call"]
+        k = c[0]
+        if k == "send":
+            dst = peer(c[1], 1)
+            rid, pid, _ = topo.addr(dst)
+            en = topo.engines(core, dst)
+            per = len(en) // len(c[2])
+            if len(c[2]) == 1:
+                p = c[2][0]
+                g.remote_dma(ap(p[1]), ap(p[0]), T.sem[p[2]], T.sem.loc, pid, rid, topo.mask(core, dst))
+            else:
+                g.remote_dma_fused([RemoteDMATransfer(dst_ids=[DstId(rid=rid, pnc=pid)],
+                                                      dma_engine_mask=sum(1 << x for x in en[j * per:(j + 1) * per]),
+                                                      remote_sem=T.sem[p[2]], src=ap(p[0]), dst=ap(p[1]))
+                                    for j, p in enumerate(c[2])], local_sem=T.sem.loc)
+            sent += per * len(c[2])
+            continue
+        if k == "ts":
+            if c[6] is None:
+                ins = e.tensor_scalar(ap(c[1]), ap(c[2]), ap(c[3]), None, c[5])
+            else:
+                ins = e.tensor_scalar(ap(c[1]), ap(c[2]), ap(c[3]), ap(c[4]), c[5], c[6])
+        elif k == "tt":
+            ins = e.tensor_tensor(ap(c[1]), ap(c[2]), ap(c[3]), c[4])
+        elif k == "cp":
+            ins = e.tensor_copy(ap(c[1]), ap(c[2]))
+        elif k == "red":
+            ins = e.tensor_reduce(ap(c[1]), ap(c[2]), AX.X, c[3])
+        elif k == "scan":
+            ins = e.tensor_tensor_scan(ap(c[1]), ap(c[2]), ap(c[3]), ap(c[4]), c[5], c[6])
+        elif k == "act":
+            kw = {}
+            if c[4] != 0.0:
+                kw["bias"] = ap(c[4])
+            if c[5] != 1.0:
+                kw["scale"] = ap(c[5])
+            if c[6]:
+                kw["accum_out"] = ap(c[6])
+            ins = e.activation(ap(c[1]), ap(c[2]), c[3], **kw)
+        elif k == "gat":
+            src = ap(c[2]).indirect(ap(c[3]))
+            ins = e.tensor_copy(ap(c[1]), src) if o["eng"] == "v" else e.activation(ap(c[1]), src, AF.Copy)
+        elif k == "iota":
+            if SCRATCH[c[1][0]][2] == "int32":
+                ins = e.iota(ap(c[1]), c[2], c[3], c[4])
+            else:
+                ins = e.iota(ap(c[1]), c[2], c[3], c[4], allow_small_or_imprecise_dtypes=True)
+        elif k == "mm":
+            for p in c[1]:
+                ins = e.matmul(ap(p[0]), ap(p[1]), ap(p[2]), p[3], p[4])
+        else:
+            ins = e.dma_start(ap(c[1]), ap(c[2]))
+        ins.then_inc(T.sem[o["done"][0]], 16 if k == "dma" else 1)
+    for en in ENG:
+        g.wait_ge(T.sem["c" + en], count[en])
+    g.wait_ge(T.sem.loc, sent)
+    for s in ("o0", "o1", "o2", "o3"):
+        g.wait_ge(T.sem[s], 16)

@@ -7,10 +7,10 @@ SCRATCH = {"bk": ("sbuf", [128, 4096], "bfloat16"), "win": ("sbuf", [128, RO * N
            "dg": ("sbuf", [128, 2048], "float16"), "nih": ("sbuf", [128, 128], "float16")}
 for _n, _w in dict(ai=256, li=4, ti=4, par=256, pi=4).items():
     SCRATCH[_n] = ("sbuf", [128, _w], "int32")
-for _n, _w in dict(ysb=256, ynb=4, yab=4, sg=256, vp=256, thf=4, thm=64, pf=4, col=144, d16=16, i32=128, kn=48, kh=48,
+for _n, _w in dict(ysb=256, ynb=4, yab=4, sg=256, vp=256, thf=4, thm=64, pf=4, col=144, d16=16, kn=48, kh=48, i32=128,
                    c2=2, c3=2, zer=48, m15=52).items():
     SCRATCH[_n] = ("sbuf", [128, _w], "float32")
-for _n, _w in dict(cg=128, ib=128, nib=128, big=128, one=128, non=128, zsel=144, kk=96, kl=96).items():
+for _n, _w in dict(cg=128, ib=128, nib=128, big=128, one=128, non=128, zsel=144, kk=96, kl=48).items():
     SCRATCH[_n] = ("sbuf", [128, _w], "bfloat16")
 for _q in range(NQ):
     SCRATCH.update({
@@ -29,10 +29,9 @@ ENG = ["v", "s", "p", "g"]
 SEMAPHORES = (["cv", "cs", "cp", "cg", "loc", "la", "lb", "ll", "lt", "o0", "o1", "o2", "o3"]
               + ["a%s%d%d" % (x, t, q) for x in "re" for t in range(RO) for q in range(NQ)])
 
-COST = dict(cy=1.04, pcy=0.52, gam=1.56, fix=25.0, hop=70.0, rem=2800.0, bank=6000.0, add=0.0)
-GUESS = [COST, dict(COST, cy=0.83, pcy=0.42, gam=1.04, fix=0.0, hop=40.0, rem=2000.0, bank=4000.0),
-         dict(COST, cy=1.25, pcy=0.62, gam=2.08, hop=120.0, rem=3500.0)]
-OPT = dict(pen="s", gate="s", dist="mm", red="v", merge=0, split=1, js=2, two=0, skew=2500.0, slack=45.0, iters=12000, temp=0.002)
+COST = dict(cy=0.83, pcy=0.42, gam=1.56, fix=15.0, hop=200.0, rem=2800.0, bank=6000.0)
+GUESS = [COST, dict(COST, cy=1.1, pcy=0.55, gam=1.9, rem=4000.0), dict(COST, hop=120.0, rem=4500.0)]
+OPT = dict(gate="s", js=3, skew=2500.0, slack=45.0, shakes=900, iters=6000, temp=0.001)
 S = 2.0 ** -21
 
 
@@ -56,7 +55,7 @@ def build_ops(C, O):
         return SCRATCH[r[0]][2] in ("bfloat16", "float16", "uint16")
 
     def vc(x):
-        return (max(64.0, x) if not C["add"] else C["add"] + x) * C["cy"] + C["fix"]
+        return max(64.0, x) * C["cy"] + C["fix"]
 
     def ts(out, in0, a, b, op0, op1=None):
         c = vc(n(out) * (0.5 if two(out) and two(in0) else 1))
@@ -86,7 +85,7 @@ def build_ops(C, O):
         return add("g", ("iota", out, pat, base, ch), [], [out], 160 + 2 * n(out) * C["cy"])
 
     def mm(parts, after=()):
-        c = sum(max(64, n(p[2])) * (4 if SCRATCH[p[2][0]][2] == "float32" else 1) for p in parts) * C["pcy"] + C["fix"]
+        c = sum(max(64, n(p[2])) * (1 if two(p[2]) else 4) for p in parts) * C["pcy"] + C["fix"]
         return add("p", ("mm", parts), [p[1] for p in parts] + [p[2] for p in parts], [p[0] for p in parts], c, after)
 
     def dma(queue, sem, out, a, reads, writes, lat, soft=()):
@@ -112,19 +111,17 @@ def build_ops(C, O):
     cp(R("pf", 1, 3), R("pi", 1, 3))
     ts(R("pf", 3, 4), R("pf", 1, 2), 16.0, 15.0, OP.mult, OP.add)
     ts(R("d16", 0, 16), R("col", 0, 16), R("pf", 2, 3), None, OP.is_equal)
-    ts(R("i32", 0, 128), R("col", 0, 128), R("pf", 0, 1), None, OP.is_equal)
-    ts(R("nih", 0, 128), R("col", 0, 128), R("pf", 0, 1), -1.0, OP.is_equal, OP.mult)
-    act(R("ib", 0, 128), R("i32", 0, 128), AF.Copy)
-    act(R("nib", 0, 128), R("i32", 0, 128), AF.Copy, scale=-1.0)
-    act(R("big", 0, 128), R("i32", 0, 128), AF.Copy, scale=0.25 if O["pen"] == "s" else -0.25)
+    ts(R("ib", 0, 128), R("col", 0, 128), R("pf", 0, 1), None, OP.is_equal)
+    act(R("nib", 0, 128), R("ib", 0, 128), AF.Copy, scale=-1.0)
+    act(R("big", 0, 128), R("ib", 0, 128), AF.Copy, scale=0.25)
+    act(R("i32", 0, 128), R("ib", 0, 128), AF.Copy)
+    ts(R("nih", 0, 128), R("ib", 0, 128), -1.0, None, OP.mult)
     ts(R("one", 0, 128), R("cg", 0, 128), R("pf", 1, 2), None, OP.is_equal)
-    if O["dist"] == "mm":
-        act(R("non", 0, 128), R("one", 0, 128), AF.Copy, scale=-1.0)
+    act(R("non", 0, 128), R("one", 0, 128), AF.Copy, scale=-1.0)
     ts(R("zsel", 0, 144), R("col", 0, 144), R("pf", 3, 4), S, OP.is_equal, OP.mult)
     act(R("kk", 0, 48), R("col", 16, 64), AF.Copy, scale=1.0 / 128)
     act(R("kk", 48, 96), R("col", 16, 64), AF.Identity, scale=-S, bias=63 * S)
     act(R("kl", 0, 48), R("col", 16, 64), AF.Copy, scale=0.0)
-    act(R("kl", 48, 96), R("col", 16, 64), AF.Identity, scale=-S, bias=63 * S)
     act(R("kh", 0, 48), R("col", 16, 64), AF.Identity, bias=0.5)
     act(R("c3", 0, 2), R("col", 0, 2), AF.Identity, scale=2.0 - 1.0 / 128, bias=1.0 / 128)
     act(R("zer", 0, 48), R("col", 0, 48), AF.Copy, scale=0.0)
@@ -149,7 +146,7 @@ def build_ops(C, O):
     act(R("vp", 0, 256), R("ysb", 0, 256), AF.Identity, bias=1.5)
     tt(R("sg", 0, 256), R("sg", 0, 256), R("vp", 0, 256), OP.mult)
     act(R("sg", 0, 256), R("sg", 0, 256), AF.Identity, bias=-0.25)
-    cp(R("thf", 0, 4), R("ti", 0, 4))
+    ts(R("thf", 0, 4), R("ti", 0, 4), 8192.0, -1.0, OP.add, OP.mult)
     for q in range(NQ):
         b = q * WW
         f, sm, of = "f%d" % q, "sm%d" % q, "of%d" % q
@@ -162,7 +159,7 @@ def build_ops(C, O):
         gat("s" if q % 2 else "v", R("win", b + 12, b + 28), R("bk", 0, 4096), R(of, 100, 101))
         ts(R(f, 336, 400), R("col", 0, 64), nn, None, OP.is_lt)
         tt(R("win", b + 32, b + 96), R(f, 336, 400), R("sg", q, 256, 4), OP.mult)
-        act(R("thm", 16 * q, 16 * q + 16), R("d16", 0, 16), AF.Copy, scale=R("thf", q, q + 1))
+        act(R("thm", 16 * q, 16 * q + 16), R("d16", 0, 16), AF.Identity, scale=R("thf", q, q + 1), bias=8192.0)
         act(R(f, 224, 239), R("ysb", q, 60, 4), AF.Identity, bias=-136.5 * S, scale=S, acc=R(sm, 26, 27))
         act(R(f, 52, 53), R("vp", 60 + q, 61 + q), AF.Copy, scale=S)
         act(R(f, 104, 105), R("vp", 60 + q, 61 + q), AF.Identity, bias=-131120.0, scale=32.0)
@@ -171,6 +168,7 @@ def build_ops(C, O):
     for name, lo, hi in (("ar0", 28, 96), ("ae0", 12, 28)):
         send(0, [(R("win", q * WW + lo, q * WW + hi), R("win", q * WW + lo + 132, q * WW + hi + 132), "%s%d" % (name, q))
                  for q in range(NQ)])
+    done = [[] for q in range(NQ)]
     for t in range(RO):
         for q in range(NQ):
             tag[0] = t * NQ + q
@@ -182,30 +180,22 @@ def build_ops(C, O):
             nn, ns = R("win", b + 28, b + 29), R("win", b + 160, b + 161)
             e, es = R("win", b + 12, b + 28), R("win", b + 144, b + 160)
             last = t == RO - 1
-            if O["dist"] == "mm":
-                tt(R(mx_, 0, 16), e, es, OP.max)
-                tt(R(mx_, 16, 32), e, es, OP.min)
-                mm([(R(ps, 64, 80), R("one", 0, 128), R(mx_, 0, 16), True, False),
-                    (R(ps, 64, 80), R("non", 0, 128), R(mx_, 16, 32), False, True)])
-            else:
-                tt(R(mx_, 0, 16), e, es, OP.subtract)
-                act(R(mx_, 16, 32), R(mx_, 0, 16), AF.Abs)
-                mm([(R(ps, 64, 80), R("one", 0, 128), R(mx_, 16, 32), True, True)])
+            tt(R(mx_, 0, 16), e, es, OP.max)
+            tt(R(mx_, 16, 32), e, es, OP.min)
+            mm([(R(ps, 64, 80), R("i32", 0, 128), R("thm", 16 * q, 16 * q + 16), True, False)], after=done[q])
+            mm([(R(ps, 64, 80), R("one", 0, 128), R(mx_, 0, 16), False, False),
+                (R(ps, 64, 80), R("non", 0, 128), R(mx_, 16, 32), False, True)])
             ts(R(sm, 16, 18), R("c2", 0, 2), ns, nn, OP.add, OP.subtract)
-            lt = tt(R(sm, 0, 16), R(ps, 64, 80), R("thm", 16 * q, 16 * q + 16), OP.is_lt)
-            if O["red"] == "v":
-                red(R(sm, 18, 19), R(sm, 0, 16), OP.add)
-            else:
-                act(R(sm, 0, 16), R(sm, 0, 16), AF.Copy, acc=R(sm, 18, 19))
-            ts(R(sm, 20, 22), R(sm, 16, 18), R(sm, 18, 19), R(sm, 23, 24), OP.mult, OP.add)
-            ts(R(of, 0, 48), R("kn", 0, 48), R(sm, 20, 21), None, OP.add)
-            if O["pen"] == "s":
-                act(R(pen, 0, 48), R("kh", 0, 48), AF.Sign, bias=R(sm, 21, 22), scale=-1.0)
-            else:
-                ts(R(pen, 0, 48), R("kh", 0, 48), R(sm, 21, 22), None, OP.is_gt)
+            lt = red(R(sm, 18, 19), R(ps, 64, 80), OP.min)
+            ts(R(sm, 20, 21), R(sm, 18, 19), 0.0, R(sm, 16, 17), OP.is_lt, OP.mult)
+            ts(R(of, 0, 48), R("kn", 0, 48), R(sm, 20, 21), R(sm, 23, 24), OP.add, OP.add)
+            ts(R(sm, 21, 22), R(sm, 18, 19), 0.0, R(sm, 17, 18), OP.is_lt, OP.mult)
+            act(R(f, 400, 448), R("kh", 0, 48), AF.Identity, bias=R(sm, 23, 24), scale=-1.0)
+            act(R(pen, 0, 48), R(f, 400, 448), AF.Sign, bias=R(sm, 21, 22))
             js = O["js"]
             for a in range(js):
-                gat("v", R(gj, 768 // js * a, 768 // js * (a + 1)), R("win", b, b + 276), R(of, 48 // js * a, 48 // js * (a + 1)))
+                lo, hi = 768 // js * a, 768 // js * (a + 1)
+                gat("v", R(gj, lo, hi), R("win", b, b + 276), R(of, lo // 16, hi // 16))
             mm([(R(ps, 0, 64), R("i32", 0, 128), R("win", b + 32, b + 96), True, False)], after=[lt])
             mm([(R(ps, 16, 64), R("dg", 128 * i, 128 * i + 128), R(gj, i, 768, 16), False, i == 15) for i in range(16)])
             act(R(f, 53, 101), R(ps, 16, 64), AF.Abs, bias=0.5 * S, scale=2.0 * S)
@@ -217,11 +207,8 @@ def build_ops(C, O):
             tt(R(xi, 0, 49), R(ps, 192, 241), R(f, 104, 153), OP.add)
             ts(R(xi, 64, 113), R(xi, 0, 49), 5, 4095, OP.arith_shift_right, OP.bitwise_and)
             prev = cp(R(of, 48, 97), R(xi, 64, 113))
-            if O["split"]:
-                gat("s", R(rx, 0, 416), R("bk", 0, 4096), R(of, 48, 74))
-                gat("s", R(rx, 416, 784), R("bk", 0, 4096), R(of, 74, 97))
-            else:
-                gat("s", R(rx, 0, 784), R("bk", 0, 4096), R(of, 48, 97))
+            gat("s", R(rx, 0, 416), R("bk", 0, 4096), R(of, 48, 74))
+            gat("s", R(rx, 416, 784), R("bk", 0, 4096), R(of, 74, 97))
             if not last:
                 prev = mm([(R(ps, 368, 416), R("i32", 0, 128), R(f, 52, 100), True, False),
                            (R(ps, 368, 416), R("ib", 0, 128), R("kk", 0, 48), False, True)], after=[prev])
@@ -233,18 +220,13 @@ def build_ops(C, O):
                 mm([(R(pdx, 0, 384), R("ib", 0, 128), R(rx, lo + 16, lo + 400), True, False),
                     (R(pdx, 0, 384), R("nib", 0, 128), R(rx, lo, lo + 384), False, True)])
                 act(R(rx, 784 + lo, 784 + lo + 384), R(pdx, 0, 384), AF.Abs, scale=64.0)
-            kt = "kl" if last else "kk"
-            if O["merge"]:
-                mm([(R(ps, 256, 352), R("ib", 0, 128), R(kt, 0, 96), True, False),
-                    (R(ps, 304, 352), R("big", 0, 128), R(pen, 0, 48), False, False)], after=[prev])
-                mm([(R(ps, 256, 352), R("zsel", 15 - i, 143 - i), R(rx, 16 + i, 1552, 16), False, i == 15) for i in range(16)])
-            else:
-                tg = mm([(R(ps, 256, 304), R("ib", 0, 128), R(kt, 0, 48), True, False)]
-                        + [(R(ps, 256, 304), R("zsel", 15 - i, 143 - i), R(rx, 16 + i, 784, 16), False, i == 15) for i in range(16)],
-                        after=[prev])
-                mm([(R(ps, 304, 352), R("ib", 0, 128), R(kt, 48, 96), True, False),
-                    (R(ps, 304, 352), R("big", 0, 128), R(pen, 0, 48), False, False)], after=[tg])
-                mm([(R(ps, 304, 352), R("zsel", 15 - i, 143 - i), R(rx, 784 + i, 1552, 16), False, i == 15) for i in range(16)])
+            tg = mm([(R(ps, 256, 304), R("ib", 0, 128), R("kl" if last else "kk", 0, 48), True, False)]
+                    + [(R(ps, 256, 304), R("zsel", 15 - i, 143 - i), R(rx, 16 + i, 784, 16), False, i == 15) for i in range(16)],
+                    after=[prev])
+            mm([(R(ps, 304, 352), R("ib", 0, 128), R("kk", 48, 96), True, False),
+                (R(ps, 304, 352), R("big", 0, 128), R(pen, 0, 48), False, False)], after=[tg])
+            done[q] = [mm([(R(ps, 304, 352), R("zsel", 15 - i, 143 - i), R(rx, 784 + i, 1552, 16), False, i == 15)
+                           for i in range(16)])]
             scan(R(f, 288, 336), R(ps, 304, 352), R("zer", 0, 48), 0.0, OP.max, OP.add)
             top = R(f, 335, 336)
             n2 = R("ynb", q, q + 1) if last else R("win", b2 + 28, b2 + 29)
@@ -255,8 +237,7 @@ def build_ops(C, O):
                 ts(R(of, 100, 101), R(f, 575, 576), R(sm, 22, 23), 1.0 / S, OP.subtract, OP.mult)
                 gat(O["gate"], R("win", b2 + 12, b2 + 28), R("bk", 0, 4096), R(of, 100, 101))
                 tt(R("win", b2 + 32, b2 + 96), R(ps, 0, 64), R(f, 336, 400), OP.mult)
-                for x, lo, hi in ((("r", 28, 96), ("e", 12, 28)) if O["two"] else (("r", 12, 96),)):
-                    send(t + 1, [(R("win", b2 + lo, b2 + hi), R("win", b2 + lo + 132, b2 + hi + 132), "a%s%d%d" % (x, t + 1, q))])
+                send(t + 1, [(R("win", b2 + 12, b2 + 96), R("win", b2 + 144, b2 + 228), "ar%d%d" % (t + 1, q))])
                 scan(R(f, 4 - t, 52 - t), R(f, 351, 399), R(ps, 256, 304), 0.0, OP.max, OP.min)
             else:
                 tt(R("ysb", 64 + q, 256, 4), R(f, 464, 512), R(f, 352, 400), OP.mult)
@@ -295,13 +276,13 @@ def greedy(ops, hop, O):
     for o in reversed(ops):
         own = -O["skew"] * (o["tag"] % NQ) if o["tag"] >= (RO - 1) * NQ else -1e9
         o["prio"] = o["cost"] + o["lat"] + hop + max([ops[u]["prio"] for u in users[o["i"]] if ops[u]["tag"] >= 0] + [own])
-    free, bank, order = {}, {}, []
+    free, order = {}, []
     left = [len(o["deps"] | o["soft"]) for o in ops]
     ready = [o for o in ops if not left[o["i"]]]
 
     def start(o):
         s = free.get(o["eng"], 0.0)
-        for j in list(o["deps"]) + [j for bk in o["banks"] for e2, j in bank.get(bk, {}).items() if e2 != o["eng"]]:
+        for j in o["deps"]:
             d = ops[j]
             s = max(s, d["end"] + (0.0 if (d["eng"] == "p" and o["eng"] == "p") or o["eng"] == "r" else hop))
         return s
@@ -312,8 +293,6 @@ def greedy(ops, hop, O):
         s1, o = max([x for x in st if x[1]["eng"] == o0["eng"] and x[0] <= s0 + O["slack"]], key=lambda x: x[1]["prio"])
         free[o["eng"]] = s1 + o["cost"] if o["eng"] != "r" else 0.0
         o["end"] = s1 + o["cost"] + o["lat"]
-        for bk in o["banks"]:
-            bank.setdefault(bk, {})[o["eng"]] = o["i"]
         order.append(o["i"])
         ready.remove(o)
         for u in users[o["i"]]:
@@ -323,7 +302,71 @@ def greedy(ops, hop, O):
     return order
 
 
-def improve(ops, order, costs, hops, iters, temp, seed=1):
+def numbers(seed):
+    state = [seed]
+
+    def rnd():
+        state[0] = (state[0] * 6364136223846793005 + 1442695040888963407) % 2 ** 64
+        return (state[0] >> 11) / 2.0 ** 53
+    return rnd
+
+
+def shake(ops, seq, hop, rounds):
+    n = len(ops)
+    pre = [[(j, 0.0 if (ops[j]["eng"] == "p" and o["eng"] == "p") or o["eng"] == "r" else hop) for j in o["deps"]] for o in ops]
+    suc = [[] for _ in ops]
+    for o in ops:
+        for j in o["soft"]:
+            pre[o["i"]].append((j, -ops[j]["lat"]))
+        for j, h in pre[o["i"]]:
+            suc[j].append((o["i"], h))
+    cost, lat = [o["cost"] for o in ops], [o["lat"] for o in ops]
+
+    def justify(seq):
+        for back in (True, False):
+            busy, st = {}, [0.0] * n
+            for i in (reversed(seq) if back else seq):
+                if back:
+                    s = max([st[j] + cost[j] + h for j, h in suc[i]] + [0.0]) + lat[i]
+                else:
+                    s = max([st[j] + cost[j] + lat[j] + h for j, h in pre[i]] + [0.0])
+                if ops[i]["eng"] != "r":
+                    iv = busy.setdefault(ops[i]["eng"], [])
+                    k = len(iv)
+                    while k > 0 and iv[k - 1][1] > s:
+                        k -= 1
+                    while k < len(iv) and iv[k][0] < s + cost[i]:
+                        s = max(s, iv[k][1])
+                        k += 1
+                    iv.insert(k, (s, s + cost[i]))
+                st[i] = s
+            place = {i: k for k, i in enumerate(seq)}
+            seq = sorted(seq, key=lambda i: (-(st[i] + cost[i]) if back else st[i], place[i]))
+        return max(st[i] + cost[i] + lat[i] for i in seq), seq
+
+    rnd = numbers(5)
+    cur = best = justify(seq)
+    for it in range(rounds):
+        s = cur[1]
+        a, w = 60 + int(rnd() * (n - 65)), 5 + int(rnd() * 55)
+        mid = s[a:a + w]
+        one = [x for x in mid if ops[x]["tag"] == ops[s[a]]["tag"]]
+        rest = [x for x in mid if ops[x]["tag"] != ops[s[a]]["tag"]]
+        new = one + rest if rnd() < 0.5 else rest + one
+        todo, fine = set(mid), True
+        for x in new:
+            todo.discard(x)
+            fine = fine and not todo & (ops[x]["deps"] | ops[x]["soft"])
+        if fine:
+            c = justify(s[:a] + new + s[a + w:])
+            if c[0] <= cur[0] + 150:
+                cur = c
+                if c[0] < best[0]:
+                    best = c
+    return best[1]
+
+
+def improve(ops, order, costs, hops, iters, temp):
     n = len(ops)
     eng = ["vspgyr".index(o["eng"]) for o in ops]
     names = sorted(set(b for o in ops for b in o["banks"]))
@@ -371,12 +414,7 @@ def improve(ops, order, costs, hops, iters, temp, seed=1):
             i = why[i]
         return top, path
 
-    state = [seed]
-
-    def rnd():
-        state[0] = (state[0] * 6364136223846793005 + 1442695040888963407) % 2 ** 64
-        return (state[0] >> 11) / 2.0 ** 53
-
+    rnd = numbers(1)
     nm = len(costs)
     res = [run(order, m) for m in range(nm)]
     base = [r[0] for r in res]
@@ -412,7 +450,7 @@ def improve(ops, order, costs, hops, iters, temp, seed=1):
 def plan(O=OPT, G=GUESS):
     ops = build_ops(G[0], O)
     link(ops)
-    seq = greedy(ops, G[0]["hop"], O)
+    seq = shake(ops, greedy(ops, G[0]["hop"], O), G[0]["hop"], O["shakes"])
     seq, times = improve(ops, seq, [[(o["cost"], o["lat"]) for o in build_ops(c, O)] for c in G], [c["hop"] for c in G],
                          O["iters"], O["temp"])
     count, known, bank = {}, {}, {}

import math
from concourse.bass import DstId, RemoteDMATransfer
from concourse.mybir import AluOpType as OP, AxisListType as AX, ActivationFunctionType as AF

RO, NQ, WW = 4, 4, 280
SCRATCH = {"bk": ("sbuf", [128, 4096], "bfloat16"), "win": ("sbuf", [128, RO * NQ * WW], "float32"),
           "dg": ("sbuf", [128, 2048], "float16"), "nih": ("sbuf", [128, 128], "float16")}
for _n, _w in dict(ai=256, li=4, ti=4, par=256, pi=4).items():
    SCRATCH[_n] = ("sbuf", [128, _w], "int32")
for _n, _w in dict(ysb=256, ynb=4, yab=4, sg=256, vp=256, thf=4, thm=64, pf=4, col=144, d16=16, kn=48, kh=48, i32=128,
                   c2=2, c3=2, zer=48, m15=52).items():
    SCRATCH[_n] = ("sbuf", [128, _w], "float32")
for _n, _w in dict(cg=128, ib=128, nib=128, big=128, one=128, non=128, zsel=144, kk=96, kl=48).items():
    SCRATCH[_n] = ("sbuf", [128, _w], "bfloat16")
for _q in range(NQ):
    SCRATCH.update({
        "sm%d" % _q: ("sbuf", [128, 32], "float32"),
        "mm%d" % _q: ("sbuf", [128, 32], "bfloat16"),
        "of%d" % _q: ("sbuf", [128, 104], "uint16"),
        "pen%d" % _q: ("sbuf", [128, 48], "bfloat16"),
        "gj%d" % _q: ("sbuf", [128, 768], "float16"),
        "f%d" % _q: ("sbuf", [128, 576], "float32"),
        "xi%d" % _q: ("sbuf", [128, 128], "int32"),
        "rx%d" % _q: ("sbuf", [128, 1552], "bfloat16"),
        "ps%d" % _q: ("psum", [128, 512], "float32"),
        "pd%d" % _q: ("psum", [128, 512], "float32"),
    })
ENG = ["v", "s", "p", "g"]
SEMAPHORES = (["cv", "cs", "cp", "cg", "loc", "la", "lb", "ll", "lt", "o0", "o1", "o2", "o3"]
              + ["a%s%d%d" % (x, t, q) for x in "re" for t in range(RO) for q in range(NQ)])

COST = dict(cy=0.83, pcy=0.42, gam=1.56, fix=15.0, hop=200.0, rem=2800.0, bank=6000.0)
GUESS = [COST, dict(COST, cy=1.1, pcy=0.55, gam=1.9, rem=4000.0), dict(COST, hop=120.0, rem=4500.0)]
OPT = dict(gate="s", js=3, skew=2500.0, slack=45.0, shakes=900, iters=6000, temp=0.001)
S = 2.0 ** -21


def R(name, lo, hi, step=1):
    return (name, lo, hi, step)


def build_ops(C, O):
    ops = []
    tag = [0]

    def add(eng, call, reads, writes, cost, after=(), sem=None, lat=0.0, soft=()):
        ops.append(dict(i=len(ops), eng=eng, call=call, reads=[r for r in reads if isinstance(r, tuple)], writes=writes,
                        cost=cost, after=list(after), sem=sem, lat=lat, tag=tag[0], soft=set(soft)))
        return len(ops) - 1

    def n(r):
        return len(range(r[1], r[2], r[3]))

    def two(r):
        return SCRATCH[r[0]][2] in ("bfloat16", "float16", "uint16")

    def vc(x):
        return max(64.0, x) * C["cy"] + C["fix"]

    def ts(out, in0, a, b, op0, op1=None):
        c = vc(n(out) * (0.5 if two(out) and two(in0) else 1))
        return add("v", ("ts", out, in0, a, b, op0, op1), [in0, a, b], [out], c)

    def tt(out, a, b, op):
        ps = SCRATCH[a[0]][0] == "psum" or SCRATCH[b[0]][0] == "psum"
        return add("v", ("tt", out, a, b, op), [a, b], [out], vc(n(out) * (1 if ps else 2)))

    def cp(out, a):
        return add("v", ("cp", out, a), [a], [out], vc(n(out)))

    def red(out, a, op):
        return add("v", ("red", out, a, op), [a], [out], vc(n(a)))

    def scan(out, a, b, init, op0, op1):
        return add("v", ("scan", out, a, b, init, op0, op1), [a, b, init], [out], vc(n(out)))

    def act(out, a, f, bias=0.0, scale=1.0, acc=None):
        return add("s", ("act", out, a, f, bias, scale, acc), [a, bias, scale], [out] + ([acc] if acc else []),
                   vc(n(out)) + (20 if acc else 0))

    def gat(eng, out, w, off):
        return add(eng, ("gat", out, w, off), [w, off], [out], n(out) * C["gam"] * C["cy"] + 65)

    def iota(out, pat, base, ch):
        return add("g", ("iota", out, pat, base, ch), [], [out], 160 + 2 * n(out) * C["cy"])

    def mm(parts, after=()):
        c = sum(max(64, n(p[2])) * (1 if two(p[2]) else 4) for p in parts) * C["pcy"] + C["fix"]
        return add("p", ("mm", parts), [p[1] for p in parts] + [p[2] for p in parts], [p[0] for p in parts], c, after)

    def dma(queue, sem, out, a, reads, writes, lat, soft=()):
        return add(queue, ("dma", out, a), reads, writes, 60.0, sem=(sem, 16), lat=lat, soft=soft)

    def send(t, parts):
        i = add("g", ("send", t, parts), [p[0] for p in parts], [], 300.0 + 30 * len(parts))
        for p in parts:
            add("r", None, [], [p[1]], 0.0, after=[i], sem=(p[2], -len(parts)), lat=C["rem"] - 500 + 6 * n(p[0]) * len(parts))

    i = dma("y", "la", R("ai", 0, 256), ("arms", 0, 256), [], [R("ai", 0, 256)], 2300.0)
    dma("y", "lb", R("bk", 0, 4096), ("bank", 0, 4096), [], [R("bk", 0, 4096)], C["bank"], soft=[i])
    i = dma("s", "ll", R("li", 0, 4), ("len0", 0, 4), [], [R("li", 0, 4)], 2100.0)
    dma("s", "lt", R("ti", 0, 4), ("th", 0, 4), [], [R("ti", 0, 4)], 2100.0, soft=[i])
    iota(R("col", 0, 144), [[1, 144]], 0, 0)
    iota(R("pi", 0, 1), [[0, 1]], 0, 1)
    iota(R("pf", 0, 1), [[0, 1]], 0, 1)
    iota(R("cg", 0, 128), [[1, 8], [0, 16]], 0, 0)
    iota(R("kn", 0, 48), [[-1, 48]], 15, 0)
    iota(R("c2", 0, 2), [[-132, 2]], 132, 0)
    ts(R("pi", 1, 2), R("pi", 0, 1), 4, None, OP.arith_shift_right)
    ts(R("pi", 2, 3), R("pi", 0, 1), 15, None, OP.bitwise_and)
    cp(R("pf", 1, 3), R("pi", 1, 3))
    ts(R("pf", 3, 4), R("pf", 1, 2), 16.0, 15.0, OP.mult, OP.add)
    ts(R("d16", 0, 16), R("col", 0, 16), R("pf", 2, 3), None, OP.is_equal)
    ts(R("ib", 0, 128), R("col", 0, 128), R("pf", 0, 1), None, OP.is_equal)
    act(R("nib", 0, 128), R("ib", 0, 128), AF.Copy, scale=-1.0)
    act(R("big", 0, 128), R("ib", 0, 128), AF.Copy, scale=0.25)
    act(R("i32", 0, 128), R("ib", 0, 128), AF.Copy)
    ts(R("nih", 0, 128), R("ib", 0, 128), -1.0, None, OP.mult)
    ts(R("one", 0, 128), R("cg", 0, 128), R("pf", 1, 2), None, OP.is_equal)
    act(R("non", 0, 128), R("one", 0, 128), AF.Copy, scale=-1.0)
    ts(R("zsel", 0, 144), R("col", 0, 144), R("pf", 3, 4), S, OP.is_equal, OP.mult)
    act(R("kk", 0, 48), R("col", 16, 64), AF.Copy, scale=1.0 / 128)
    act(R("kk", 48, 96), R("col", 16, 64), AF.Identity, scale=-S, bias=63 * S)
    act(R("kl", 0, 48), R("col", 16, 64), AF.Copy, scale=0.0)
    act(R("kh", 0, 48), R("col", 16, 64), AF.Identity, bias=0.5)
    act(R("c3", 0, 2), R("col", 0, 2), AF.Identity, scale=2.0 - 1.0 / 128, bias=1.0 / 128)
    act(R("zer", 0, 48), R("col", 0, 48), AF.Copy, scale=0.0)
    act(R("m15", 0, 3), R("col", 0, 3), AF.Copy, scale=0.0)
    act(R("m15", 3, 52), R("col", 0, 49), AF.Identity, scale=0.0, bias=-1.5 * S)
    for i in range(16):
        ts(R("dg", 128 * i, 128 * i + 128), R("nih", 0, 128), R("d16", i, i + 1), None, OP.mult)
    for w in range(RO * NQ + 1):
        b = w * WW
        tag[0] = max(w - 1, 0)
        spans = [(max(b - 52, 0), min(b + 32, RO * NQ * WW))] + ([(b + 96, b + 144)] if w < RO * NQ else [])
        for lo, hi in spans:
            if w < NQ:
                act(R("win", lo, hi), R("col", 0, hi - lo), AF.Copy, scale=0.0)
            else:
                iota(R("win", lo, hi), [[0, hi - lo]], 0, 0)
    tag[0] = 0
    cp(R("ysb", 0, 256), R("ai", 0, 256))
    dma("y", "o0", ("ys", 0, 64), R("ysb", 0, 64), [R("ysb", 0, 64)], [], 2200.0)
    ts(R("par", 0, 256), R("ai", 0, 256), 1, None, OP.bitwise_and)
    ts(R("sg", 0, 256), R("par", 0, 256), -0.5, None, OP.add)
    act(R("vp", 0, 256), R("ysb", 0, 256), AF.Identity, bias=1.5)
    tt(R("sg", 0, 256), R("sg", 0, 256), R("vp", 0, 256), OP.mult)
    act(R("sg", 0, 256), R("sg", 0, 256), AF.Identity, bias=-0.25)
    ts(R("thf", 0, 4), R("ti", 0, 4), 8192.0, -1.0, OP.add, OP.mult)
    for q in range(NQ):
        b = q * WW
        f, sm, of = "f%d" % q, "sm%d" % q, "of%d" % q
        nn = R("win", b + 28, b + 29)
        cp(nn, R("li", q, q + 1))
        ts(R(f, 400, 464), R("col", 0, 64), 1.0, nn, OP.add, OP.is_equal)
        tt(R(f, 464, 528), R(f, 400, 464), R("ysb", q, 256, 4), OP.mult)
        act(R(f, 160, 224), R(f, 464, 528), AF.Copy, acc=R(sm, 24, 25))
        cp(R(of, 100, 101), R(sm, 24, 25))
        gat("s" if q % 2 else "v", R("win", b + 12, b + 28), R("bk", 0, 4096), R(of, 100, 101))
        ts(R(f, 336, 400), R("col", 0, 64), nn, None, OP.is_lt)
        tt(R("win", b + 32, b + 96), R(f, 336, 400), R("sg", q, 256, 4), OP.mult)
        act(R("thm", 16 * q, 16 * q + 16), R("d16", 0, 16), AF.Identity, scale=R("thf", q, q + 1), bias=8192.0)
        act(R(f, 224, 239), R("ysb", q, 60, 4), AF.Identity, bias=-136.5 * S, scale=S, acc=R(sm, 26, 27))
        act(R(f, 52, 53), R("vp", 60 + q, 61 + q), AF.Copy, scale=S)
        act(R(f, 104, 105), R("vp", 60 + q, 61 + q), AF.Identity, bias=-131120.0, scale=32.0)
        act(R(f, 272, 288), R("col", 0, 16), AF.Identity, scale=0.0, bias=-1.0)
        act(R(sm, 22, 24), R("c3", 0, 2), AF.Identity, scale=nn, bias=1.5 * S)
    for name, lo, hi in (("ar0", 28, 96), ("ae0", 12, 28)):
        send(0, [(R("win", q * WW + lo, q * WW + hi), R("win", q * WW + lo + 132, q * WW + hi + 132), "%s%d" % (name, q))
                 for q in range(NQ)])
    done = [[] for q in range(NQ)]
    for t in range(RO):
        for q in range(NQ):
            tag[0] = t * NQ + q
            b = (t * NQ + q) * WW
            b2 = b + NQ * WW
            f, sm, of, ps = "f%d" % q, "sm%d" % q, "of%d" % q, "ps%d" % q
            mx_, gj, xi, rx, pen = "mm%d" % q, "gj%d" % q, "xi%d" % q, "rx%d" % q, "pen%d" % q
            pa, pb = "pd%d" % (2 * (q % 2)), "pd%d" % (2 * (q % 2) + 1)
            nn, ns = R("win", b + 28, b + 29), R("win", b + 160, b + 161)
            e, es = R("win", b + 12, b + 28), R("win", b + 144, b + 160)
            last = t == RO - 1
            tt(R(mx_, 0, 16), e, es, OP.max)
            tt(R(mx_, 16, 32), e, es, OP.min)
            mm([(R(ps, 64, 80), R("i32", 0, 128), R("thm", 16 * q, 16 * q + 16), True, False)], after=done[q])
            mm([(R(ps, 64, 80), R("one", 0, 128), R(mx_, 0, 16), False, False),
                (R(ps, 64, 80), R("non", 0, 128), R(mx_, 16, 32), False, True)])
            ts(R(sm, 16, 18), R("c2", 0, 2), ns, nn, OP.add, OP.subtract)
            lt = red(R(sm, 18, 19), R(ps, 64, 80), OP.min)
            ts(R(sm, 20, 21), R(sm, 18, 19), 0.0, R(sm, 16, 17), OP.is_lt, OP.mult)
            ts(R(of, 0, 48), R("kn", 0, 48), R(sm, 20, 21), R(sm, 23, 24), OP.add, OP.add)
            ts(R(sm, 21, 22), R(sm, 18, 19), 0.0, R(sm, 17, 18), OP.is_lt, OP.mult)
            act(R(f, 400, 448), R("kh", 0, 48), AF.Identity, bias=R(sm, 23, 24), scale=-1.0)
            act(R(pen, 0, 48), R(f, 400, 448), AF.Sign, bias=R(sm, 21, 22))
            js = O["js"]
            for a in range(js):
                lo, hi = 768 // js * a, 768 // js * (a + 1)
                gat("v", R(gj, lo, hi), R("win", b, b + 276), R(of, lo // 16, hi // 16))
            mm([(R(ps, 0, 64), R("i32", 0, 128), R("win", b + 32, b + 96), True, False)], after=[lt])
            mm([(R(ps, 16, 64), R("dg", 128 * i, 128 * i + 128), R(gj, i, 768, 16), False, i == 15) for i in range(16)])
            act(R(f, 53, 101), R(ps, 16, 64), AF.Abs, bias=0.5 * S, scale=2.0 * S)
            scan(R(ps, 128 - t, 177), R(f, 52 - t, 101), R("m15", 3 - t, 52), R(sm, 26, 27), OP.add, OP.add)
            act(R(f, 105, 153), R(f, 53, 101), AF.Identity, bias=-131120.0, scale=32.0 / S)
            ts(R(f, 160, 209), R(ps, 128, 177), 1.5 * 2.0 ** 35 * S, 1.5 * 2.0 ** 35 * S, OP.add, OP.subtract)
            tt(R(f, 216, 265), R(ps, 128, 177), R(f, 160, 209), OP.subtract)
            act(R(ps, 192, 241), R(f, 216, 265), AF.Square, bias=2047.5, scale=1.0 / S)
            tt(R(xi, 0, 49), R(ps, 192, 241), R(f, 104, 153), OP.add)
            ts(R(xi, 64, 113), R(xi, 0, 49), 5, 4095, OP.arith_shift_right, OP.bitwise_and)
            prev = cp(R(of, 48, 97), R(xi, 64, 113))
            gat("s", R(rx, 0, 416), R("bk", 0, 4096), R(of, 48, 74))
            gat("s", R(rx, 416, 784), R("bk", 0, 4096), R(of, 74, 97))
            if not last:
                prev = mm([(R(ps, 368, 416), R("i32", 0, 128), R(f, 52, 100), True, False),
                           (R(ps, 368, 416), R("ib", 0, 128), R("kk", 0, 48), False, True)], after=[prev])
            else:
                act(R(f, 400, 403), R(f, 49, 52), AF.Identity, bias=2730.5 * S, scale=-1.0, acc=R(sm, 24, 25))
                ts(R(f, 48, 49), R(sm, 24, 25), 1.5 * 2.0 ** 37 * S, 1.5 * 2.0 ** 37 * S, OP.add, OP.subtract)
                act(R(f, 464, 512), R(f, 53, 101), AF.Identity, bias=-1.5, scale=1.0 / S)
            for pdx, lo in ((pa, 0), (pb, 384)):
                mm([(R(pdx, 0, 384), R("ib", 0, 128), R(rx, lo + 16, lo + 400), True, False),
                    (R(pdx, 0, 384), R("nib", 0, 128), R(rx, lo, lo + 384), False, True)])
                act(R(rx, 784 + lo, 784 + lo + 384), R(pdx, 0, 384), AF.Abs, scale=64.0)
            tg = mm([(R(ps, 256, 304), R("ib", 0, 128), R("kl" if last else "kk", 0, 48), True, False)]
                    + [(R(ps, 256, 304), R("zsel", 15 - i, 143 - i), R(rx, 16 + i, 784, 16), False, i == 15) for i in range(16)],
                    after=[prev])
            mm([(R(ps, 304, 352), R("ib", 0, 128), R("kk", 48, 96), True, False),
                (R(ps, 304, 352), R("big", 0, 128), R(pen, 0, 48), False, False)], after=[tg])
            done[q] = [mm([(R(ps, 304, 352), R("zsel", 15 - i, 143 - i), R(rx, 784 + i, 1552, 16), False, i == 15)
                           for i in range(16)])]
            scan(R(f, 288, 336), R(ps, 304, 352), R("zer", 0, 48), 0.0, OP.max, OP.add)
            top = R(f, 335, 336)
            n2 = R("ynb", q, q + 1) if last else R("win", b2 + 28, b2 + 29)
            act(R(f, 336, 400), R(f, 272, 336), AF.Sign, bias=top, scale=-1.0, acc=n2)
            if not last:
                act(R(sm, 22, 24), R("c3", 0, 2), AF.Identity, scale=n2, bias=1.5 * S)
                scan(R(f, 528, 576), R(f, 351, 399), R(ps, 368, 416), 0.0, OP.max, OP.min)
                ts(R(of, 100, 101), R(f, 575, 576), R(sm, 22, 23), 1.0 / S, OP.subtract, OP.mult)
                gat(O["gate"], R("win", b2 + 12, b2 + 28), R("bk", 0, 4096), R(of, 100, 101))
                tt(R("win", b2 + 32, b2 + 96), R(ps, 0, 64), R(f, 336, 400), OP.mult)
                send(t + 1, [(R("win", b2 + 12, b2 + 96), R("win", b2 + 144, b2 + 228), "ar%d%d" % (t + 1, q))])
                scan(R(f, 4 - t, 52 - t), R(f, 351, 399), R(ps, 256, 304), 0.0, OP.max, OP.min)
            else:
                tt(R("ysb", 64 + q, 256, 4), R(f, 464, 512), R(f, 352, 400), OP.mult)
                ts(R(f, 404, 452), R(ps, 304, 352), top, None, OP.is_equal)
                tt(R(f, 0, 48), R(ps, 256, 304), R(f, 404, 452), OP.mult)
                act(R(f, 104, 156), R(f, 0, 52), AF.Copy, scale=1.0 / S, acc=R("yab", q, q + 1))
    tag[0] = -1
    dma("y", "o1", ("ys", 64, 256), R("ysb", 64, 256), [R("ysb", 64, 256)], [], 2300.0)
    dma("y", "o2", ("yn", 0, 4), R("ynb", 0, 4), [R("ynb", 0, 4)], [], 2100.0)
    dma("s", "o3", ("ya", 0, 4), R("yab", 0, 4), [R("yab", 0, 4)], [], 2100.0)
    return ops


def link(ops):
    hist = {}
    for o in ops:
        deps = set(o["after"])
        for kind, regs in (("r", o["reads"]), ("w", o["writes"])):
            for r in regs:
                for (j, k2, lo, hi) in hist.get(r[0], []):
                    if lo < r[2] and r[1] < hi and (kind == "w" or k2 == "w"):
                        deps.add(j)
        for kind, regs in (("r", o["reads"]), ("w", o["writes"])):
            for r in regs:
                hist.setdefault(r[0], []).append((o["i"], kind, r[1], r[2]))
        deps.discard(o["i"])
        o["deps"] = deps
        o["banks"] = sorted(set(r[0] for r in o["reads"] + o["writes"] if SCRATCH[r[0]][0] == "psum"))


def greedy(ops, hop, O):
    users = [[] for _ in ops]
    for o in ops:
        for j in o["deps"] | o["soft"]:
            users[j].append(o["i"])
    for o in reversed(ops):
        own = -O["skew"] * (o["tag"] % NQ) if o["tag"] >= (RO - 1) * NQ else -1e9
        o["prio"] = o["cost"] + o["lat"] + hop + max([ops[u]["prio"] for u in users[o["i"]] if ops[u]["tag"] >= 0] + [own])
    free, order = {}, []
    left = [len(o["deps"] | o["soft"]) for o in ops]
    ready = [o for o in ops if not left[o["i"]]]

    def start(o):
        s = free.get(o["eng"], 0.0)
        for j in o["deps"]:
            d = ops[j]
            s = max(s, d["end"] + (0.0 if (d["eng"] == "p" and o["eng"] == "p") or o["eng"] == "r" else hop))
        return s

    while ready:
        st = [(start(o), o) for o in ready]
        s0, o0 = min(st, key=lambda x: (x[0], -x[1]["prio"]))
        s1, o = max([x for x in st if x[1]["eng"] == o0["eng"] and x[0] <= s0 + O["slack"]], key=lambda x: x[1]["prio"])
        free[o["eng"]] = s1 + o["cost"] if o["eng"] != "r" else 0.0
        o["end"] = s1 + o["cost"] + o["lat"]
        order.append(o["i"])
        ready.remove(o)
        for u in users[o["i"]]:
            left[u] -= 1
            if left[u] == 0:
                ready.append(ops[u])
    return order


def numbers(seed):
    state = [seed]

    def rnd():
        state[0] = (state[0] * 6364136223846793005 + 1442695040888963407) % 2 ** 64
        return (state[0] >> 11) / 2.0 ** 53
    return rnd


def shake(ops, seq, hop, rounds):
    n = len(ops)
    pre = [[(j, 0.0 if (ops[j]["eng"] == "p" and o["eng"] == "p") or o["eng"] == "r" else hop) for j in o["deps"]] for o in ops]
    suc = [[] for _ in ops]
    for o in ops:
        for j in o["soft"]:
            pre[o["i"]].append((j, -ops[j]["lat"]))
        for j, h in pre[o["i"]]:
            suc[j].append((o["i"], h))
    cost, lat = [o["cost"] for o in ops], [o["lat"] for o in ops]

    def justify(seq):
        for back in (True, False):
            busy, st = {}, [0.0] * n
            for i in (reversed(seq) if back else seq):
                if back:
                    s = max([st[j] + cost[j] + h for j, h in suc[i]] + [0.0]) + lat[i]
                else:
                    s = max([st[j] + cost[j] + lat[j] + h for j, h in pre[i]] + [0.0])
                if ops[i]["eng"] != "r":
                    iv = busy.setdefault(ops[i]["eng"], [])
                    k = len(iv)
                    while k > 0 and iv[k - 1][1] > s:
                        k -= 1
                    while k < len(iv) and iv[k][0] < s + cost[i]:
                        s = max(s, iv[k][1])
                        k += 1
                    iv.insert(k, (s, s + cost[i]))
                st[i] = s
            place = {i: k for k, i in enumerate(seq)}
            seq = sorted(seq, key=lambda i: (-(st[i] + cost[i]) if back else st[i], place[i]))
        return max(st[i] + cost[i] + lat[i] for i in seq), seq

    rnd = numbers(5)
    cur = best = justify(seq)
    for it in range(rounds):
        s = cur[1]
        a, w = 60 + int(rnd() * (n - 65)), 5 + int(rnd() * 55)
        mid = s[a:a + w]
        one = [x for x in mid if ops[x]["tag"] == ops[s[a]]["tag"]]
        rest = [x for x in mid if ops[x]["tag"] != ops[s[a]]["tag"]]
        new = one + rest if rnd() < 0.5 else rest + one
        todo, fine = set(mid), True
        for x in new:
            todo.discard(x)
            fine = fine and not todo & (ops[x]["deps"] | ops[x]["soft"])
        if fine:
            c = justify(s[:a] + new + s[a + w:])
            if c[0] <= cur[0] + 150:
                cur = c
                if c[0] < best[0]:
                    best = c
    return best[1]


def improve(ops, order, costs, hops, iters, temp):
    n = len(ops)
    eng = ["vspgyr".index(o["eng"]) for o in ops]
    names = sorted(set(b for o in ops for b in o["banks"]))
    banks = [[names.index(b) for b in o["banks"]] for o in ops]
    anc = [0] * n
    deps = []
    for o in ops:
        d = sorted(o["deps"] | o["soft"])
        deps.append([j for j in d if j not in o["soft"] and not any(anc[k] >> j & 1 for k in d)])
        for j in d:
            anc[o["i"]] |= anc[j] | 1 << j
    dep0 = [[j for j in deps[i] if (eng[i] == 2 and eng[j] == 2) or eng[i] == 5] for i in range(n)]
    dep1 = [[j for j in deps[i] if j not in dep0[i]] for i in range(n)]

    def run(seq, m):
        cost, hop = costs[m], hops[m]
        free, holder, end, why = [0.0] * 6, [-1] * 6, [0.0] * n, [-1] * n
        bank = [[-1] * 3 for _ in names]
        for i in seq:
            e = eng[i]
            s, w = (free[e], holder[e]) if e != 5 else (0.0, -1)
            for j in dep1[i]:
                if end[j] + hop > s:
                    s, w = end[j] + hop, j
            for j in dep0[i]:
                if end[j] > s:
                    s, w = end[j], j
            for b in banks[i]:
                bb = bank[b]
                for e2 in (0, 1, 2):
                    j = bb[e2]
                    if e2 != e and j >= 0 and end[j] + hop > s:
                        s, w = end[j] + hop, j
                bb[e] = i
            c = cost[i]
            free[e] = s + c[0]
            holder[e] = i
            end[i] = s + c[0] + c[1]
            why[i] = w
        top = max(end)
        i, path = end.index(top), []
        while why[i] >= 0:
            if not anc[i] >> why[i] & 1:
                path.append((why[i], i))
            i = why[i]
        return top, path

    rnd = numbers(1)
    nm = len(costs)
    res = [run(order, m) for m in range(nm)]
    base = [r[0] for r in res]
    cur = best = float(nm)
    keep = order
    for it in range(iters):
        path = res[int(rnd() * nm)][1]
        if not path:
            continue
        p, o = path[int(rnd() * len(path))]
        a, b = order.index(p), order.index(o)
        if rnd() < 0.3:
            a = max(0, a - int(rnd() * 12))
            p = order[a]
        mid = order[a:b + 1]
        if rnd() < 0.5:
            mv = [x for x in mid if x == o or anc[o] >> x & 1]
            st = set(mv)
            new = order[:a] + mv + [x for x in mid if x not in st] + order[b + 1:]
        else:
            mv = [x for x in mid if x == p or anc[x] >> p & 1]
            st = set(mv)
            new = order[:a] + [x for x in mid if x not in st] + mv + order[b + 1:]
        r2 = [run(new, m) for m in range(nm)]
        val = sum(r2[m][0] / base[m] for m in range(nm))
        if val <= cur or rnd() < math.exp((cur - val) / (nm * temp * (1.0 - it / iters) + 1e-9)):
            order, res, cur = new, r2, val
            if val < best:
                best, keep = val, new
    return keep, [int(run(keep, m)[0]) for m in range(nm)]


def plan(O=OPT, G=GUESS):
    ops = build_ops(G[0], O)
    link(ops)
    seq = shake(ops, greedy(ops, G[0]["hop"], O), G[0]["hop"], O["shakes"])
    seq, times = improve(ops, seq, [[(o["cost"], o["lat"]) for o in build_ops(c, O)] for c in G], [c["hop"] for c in G],
                         O["iters"], O["temp"])
    count, known, bank = {}, {}, {}
    place = {i: k for k, i in enumerate(seq)}
    for i in seq:
        o = ops[i]
        kn = known.setdefault(o["eng"], {})
        waits = {}
        need = set(o["deps"]) | set(j for bk in o["banks"] for e2, j in bank.get(bk, {}).items() if e2 != o["eng"])
        for bk in o["banks"]:
            bank.setdefault(bk, {})[o["eng"]] = i
        if o["eng"] != "r":
            for j in sorted(need, key=lambda j: -place[j]):
                d = ops[j]
                if d["eng"] == "p" and o["eng"] == "p":
                    continue
                s, v = d["done"]
                if kn.get(s, 0) != v and (v < 0 or kn.get(s, 0) < v):
                    waits[s] = v if v < 0 else max(v, waits.get(s, 0))
                    kn[s] = v
                    for s2, v2 in d["know"].items():
                        if v2 < 0 or kn.get(s2, 0) < v2:
                            kn[s2] = v2
        o["waits"] = waits
        o["know"] = {} if o["eng"] == "r" else dict(kn)
        if o["sem"]:
            o["done"] = o["sem"]
        elif o["call"][0] == "send":
            o["done"] = None
        else:
            count[o["eng"]] = count.get(o["eng"], 0) + 1
            o["done"] = ("c" + o["eng"], count[o["eng"]])
    return [ops[i] for i in seq], count, times


PLAN = {}


def rank_program(g, core, T, topo):
    rank = T.rank_of(core)
    if rank is None:
        return
    if "p" not in PLAN:
        PLAN["p"] = plan()
    order, count, _ = PLAN["p"]
    nr = len(T.cores)
    queue = {"v": g.vector, "s": g.scalar, "p": g.tensor, "g": g, "y": g.sync}

    def peer(t, sign):
        return T.cores[(rank + sign * (1 + t % (nr - 1))) % nr]

    def ap(r):
        if not isinstance(r, tuple):
            return r
        if len(r) == 4 and r[3] != 1:
            return T[r[0]][:, r[1]:r[2]:r[3]]
        return T[r[0]][:, r[1]:r[2]]

    def value(s, v):
        if v > 0:
            return v
        return len(topo.engines(peer(int(s[2]), -1), core)) // -v

    sent = 0
    for o in order:
        if o["eng"] == "r":
            continue
        e = queue[o["eng"]]
        for s, v in o["waits"].items():
            e.wait_ge(T.sem[s], value(s, v))
        c = o["call"]
        k = c[0]
        if k == "send":
            dst = peer(c[1], 1)
            rid, pid, _ = topo.addr(dst)
            en = topo.engines(core, dst)
            per = len(en) // len(c[2])
            if len(c[2]) == 1:
                p = c[2][0]
                g.remote_dma(ap(p[1]), ap(p[0]), T.sem[p[2]], T.sem.loc, pid, rid, topo.mask(core, dst))
            else:
                g.remote_dma_fused([RemoteDMATransfer(dst_ids=[DstId(rid=rid, pnc=pid)],
                                                      dma_engine_mask=sum(1 << x for x in en[j * per:(j + 1) * per]),
                                                      remote_sem=T.sem[p[2]], src=ap(p[0]), dst=ap(p[1]))
                                    for j, p in enumerate(c[2])], local_sem=T.sem.loc)
            sent += per * len(c[2])
            continue
        if k == "ts":
            if c[6] is None:
                ins = e.tensor_scalar(ap(c[1]), ap(c[2]), ap(c[3]), None, c[5])
            else:
                ins = e.tensor_scalar(ap(c[1]), ap(c[2]), ap(c[3]), ap(c[4]), c[5], c[6])
        elif k == "tt":
            ins = e.tensor_tensor(ap(c[1]), ap(c[2]), ap(c[3]), c[4])
        elif k == "cp":
            ins = e.tensor_copy(ap(c[1]), ap(c[2]))
        elif k == "red":
            ins = e.tensor_reduce(ap(c[1]), ap(c[2]), AX.X, c[3])
        elif k == "scan":
            ins = e.tensor_tensor_scan(ap(c[1]), ap(c[2]), ap(c[3]), ap(c[4]), c[5], c[6])
        elif k == "act":
            kw = {}
            if c[4] != 0.0:
                kw["bias"] = ap(c[4])
            if c[5] != 1.0:
                kw["scale"] = ap(c[5])
            if c[6]:
                kw["accum_out"] = ap(c[6])
            ins = e.activation(ap(c[1]), ap(c[2]), c[3], **kw)
        elif k == "gat":
            src = ap(c[2]).indirect(ap(c[3]))
            ins = e.tensor_copy(ap(c[1]), src) if o["eng"] == "v" else e.activation(ap(c[1]), src, AF.Copy)
        elif k == "iota":
            if SCRATCH[c[1][0]][2] == "int32":
                ins = e.iota(ap(c[1]), c[2], c[3], c[4])
            else:
                ins = e.iota(ap(c[1]), c[2], c[3], c[4], allow_small_or_imprecise_dtypes=True)
        elif k == "mm":
            for p in c[1]:
                ins = e.matmul(ap(p[0]), ap(p[1]), ap(p[2]), p[3], p[4])
        else:
            ins = e.dma_start(ap(c[1]), ap(c[2]))
        ins.then_inc(T.sem[o["done"][0]], 16 if k == "dma" else 1)
    for en in ENG:
        g.wait_ge(T.sem["c" + en], count[en])
    g.wait_ge(T.sem.loc, sent)
    for s in ("o0", "o1", "o2", "o3"):
        g.wait_ge(T.sem[s], 16)
